import numpy as np
import ml_dtypes


def mxq(x, axis, fmt="e4m3"):
    dtype, down = {"e4m3": (ml_dtypes.float8_e4m3fn, 7), "e5m2": (ml_dtypes.float8_e5m2, 14)}[fmt]
    v = np.moveaxis(np.asarray(x, np.float32).astype(ml_dtypes.bfloat16).astype(np.float64), axis, -1)
    blocks = v.reshape(v.shape[:-1] + (-1, 32))
    amax = np.abs(blocks).max(-1, keepdims=True)
    byte = np.maximum(np.where(amax > 0, np.frexp(amax)[1] - 1 + 127, 0) - down, 1)
    scale = np.exp2(byte - 127.0)
    codes = (blocks / scale).astype(np.float32).astype(dtype).astype(np.float64)
    return np.moveaxis((codes * scale).reshape(v.shape), -1, axis)


WIDE = False


def mx_kscale(k):
    if not WIDE:
        return np.ones(k)
    levels = np.array([10, -10, 5, -5, 0])
    if k % 512:
        return np.exp2(np.random.permutation(np.resize(levels, k // 32))).repeat(32)
    a = np.empty((k // 512, 16))
    for p in range(k // 512):
        a[p, :8] = np.random.permutation(np.resize(levels, 8))
        for g in range(8):
            far = levels[np.abs(levels - a[p, g]) >= 10]
            a[p, g + 8] = far[np.random.randint(len(far))]
    return np.exp2(a.ravel()).repeat(32)


def f64(x):
    return np.asarray(x).astype(np.float64)


def striped(idx):
    return np.tile(idx.reshape(-1, 16).T, (8, 1)).astype(np.uint16)


def unstriped(offs):
    return offs[:16].T.reshape(-1).astype(np.int64)


E2M1 = np.array([0.0, 0.5, 1.0, 1.5, 2.0, 3.0, 4.0, 6.0, -0.0, -0.5, -1.0, -1.5, -2.0, -3.0, -4.0, -6.0])


def pack_weight(w, fmt):
    k, n = w.shape
    w = f64(np.asarray(w, np.float32).astype(ml_dtypes.bfloat16)).reshape(k // 32, 32, n)
    amax = np.abs(w).max(1)
    if fmt == "e4m3":
        byte = np.frexp(amax)[1] - 1 + 127 - 7
    else:
        mant, ex = np.frexp(amax / 6.0)
        byte = np.where(mant > 0.5, ex, ex - 1) + 127
    byte = np.clip(np.where(amax > 0, byte, 1), 1, 254)
    scaled = (w * np.exp2(127.0 - byte)[:, None, :]).reshape(k, n).astype(np.float32)
    by_word = np.ascontiguousarray(scaled.reshape(k // 512, 128, 4, n).transpose(0, 1, 3, 2))
    if fmt == "e4m3":
        words = by_word.astype(ml_dtypes.float8_e4m3fn).view(np.uint8)
    else:
        c = by_word.astype(ml_dtypes.float4_e2m1fn).view(np.uint8) & 0xF
        words = (c[..., 0::2] | (c[..., 1::2] << 4)).reshape(k // 512, 128, 2 * n)
    return np.ascontiguousarray(words), np.ascontiguousarray(byte.astype(np.uint8).reshape(k // 512, 16, n))


def unpack_weight(words, scales, fmt):
    g, _, n = scales.shape
    words = np.ascontiguousarray(words).reshape(g, 128, n, -1)
    if fmt == "e4m3":
        vals = words.view(ml_dtypes.float8_e4m3fn).astype(np.float64)
    else:
        nib = np.empty((g, 128, n, 4), np.uint8)
        nib[..., 0::2] = words & 0xF
        nib[..., 1::2] = words >> 4
        vals = E2M1[nib]
    vals = vals * np.repeat(np.exp2(scales.astype(np.float64) - 127.0), 8, axis=1)[..., None]
    return vals.transpose(0, 1, 3, 2).reshape(g * 512, n)


def gelu(v):
    return 0.5 * v * (1.0 + np.tanh(np.sqrt(2.0 / np.pi) * (v + 0.044715 * v**3)))


K, H, N, T, S, T2 = 512, 1024, 512, 4096, 1024, 2048


def setup_inputs():
    n = np.random.standard_normal
    s = mx_kscale(K)[:, None]
    u = mx_kscale(H)[:, None]
    tab_words, tab_scales = pack_weight(n((K, T)) * s, "e4m3")
    wb_words, wb_scales = pack_weight(n((K, H)) / np.sqrt(K) / s, "e2m1")
    return {
        "tab_words": tab_words,
        "tab_scales": tab_scales,
        "offs": striped(np.random.permutation(T)[:S]),
        "offs2": striped(np.random.permutation(T)[:S]),
        "offs3": striped(np.random.permutation(T2)[:S]),
        "wa": (n((K, H)) / np.sqrt(K) / s).astype(np.float32),
        "wb_words": wb_words,
        "wb_scales": wb_scales,
        "airport": n((H, S)).astype(np.float32),
        "gain": (np.exp(0.3 * n(H)) * u[:, 0]).astype(np.float32),
        "wc": (n((H, N)) / np.sqrt(H) / u).astype(np.float32),
        "wgo": np.exp(0.3 * n((128, S))).astype(np.float32),
    }


def reference(tab_words, tab_scales, offs, offs2, offs3, wa, wb_words, wb_scales, airport, gain, wc, wgo):
    TW = unpack_weight(tab_words, tab_scales, "e4m3")
    v = TW[:, unstriped(offs)]
    v2 = TW[:, unstriped(offs2)]
    ap = f64(airport)
    bags = np.tanh((mxq(f64(wa), 0, "e4m3").T @ v) + ap)
    reports = (unpack_weight(wb_words, wb_scales, "e2m1").T @ v2) * ap
    z = (bags - reports) * f64(gain)[:, None]
    y = np.abs(mxq(f64(wc), 0, "e4m3").T @ mxq(z, 0, "e4m3"))
    out = np.zeros((N, T2))
    out[:, unstriped(offs3)] = np.tile(f64(wgo), (N // 128, 1)) * y
    return out

@@ -1,0 +1,393 @@
+from contextlib import ExitStack
+
+import concourse.mybir as mybir
+from concourse.masks import make_identity
+
+K, H, N, T, S, T2 = 512, 1024, 512, 4096, 1024, 2048
+FLOPS = 2 * (2 * K * H * S + H * N * S)
+
+F32 = mybir.dt.float32
+BF16 = mybir.dt.bfloat16
+I32 = mybir.dt.int32
+U32 = mybir.dt.uint32
+U16 = mybir.dt.uint16
+U8 = mybir.dt.uint8
+FP8X4 = mybir.dt.float8_e4m3fn_x4
+FP4X4 = mybir.dt.float4_e2m1fn_x4
+ALU = mybir.AluOpType
+ACT = mybir.ActivationFunctionType
+
+P = 128
+PACK = 4
+BANK = 512
+GROUPS = H // (P * PACK)
+HALF = S // 2
+CHUNKS = ((0, 256), (256, 256), (512, 256), (768, 256))
+PE_ADD = (False, True, True, True)
+GATE = "rep"
+HEAD = "rep bag bw ts tw bs gain wa0 ap00 wa1 ap01 wc0 wc1 ap10 ap11 out wgo ap20 ap21 ap30 ap31"
+WC_V = (0, 1)
+LAG = 0
+REPS = 4
+NA = 2
+NB = 1
+NBACK = 2
+YB = "y"
+RA = 3
+RBAG = 4
+JOBS = (5, 7, 9, 11, 13, 15, 15, 15)
+GH = 0
+FIN = "a"
+
+
+def tile_list_bag_report_tracing_kernel(
+    tc, tab_words, tab_scales, offs, offs2, offs3, wa, wb_words, wb_scales, airport, gain, wc, wgo, out
+):
+    nc = tc.nc
+    with ExitStack() as ctx:
+        keep = ctx.enter_context(tc.tile_pool(name="keep", bufs=1))
+        psum = ctx.enter_context(tc.psum_pool(name="psum", bufs=1))
+
+        def held(name, shape, dtype):
+            return keep.tile(shape, dtype, name=name, align_bytes=64)
+
+        def ring(name, count, shape, dtype):
+            return [held("%s%d" % (name, i), shape, dtype) for i in range(count)]
+
+        def banks(name, count):
+            return [psum.tile([P, BANK], F32, name="%s%d" % (name, i)) for i in range(count)]
+
+        bank_a = banks("bank_a", NA)
+        bank_turn = banks("bank_turn", 2)
+        bank_b = banks("bank_b", NB)
+        bank_back = banks("bank_back", NBACK)
+        bank_y = banks("bank_y", 1) if YB == "y" else None
+        ring_a = ring("a_sb", RA, [P, BANK], F32)
+        ring_bags = ring("bags", RBAG, [P, BANK], F32)
+        ring_rep = ring("rep", REPS, [P, BANK], F32)
+        ring_mag = ring("mag", 2, [P, BANK], F32)
+        ring_z = ring("z_rows", 2, [P, PACK, 256], BF16)
+        ring_zbf = ring("z_bf", 2, [P, PACK * 256], BF16)
+
+        list_bag = keep.tile([P, S // 16], U16, name="list_bag")
+        list_rep = keep.tile([P, S // 16], U16, name="list_rep")
+        list_out = keep.tile([P, S // 16], U16, name="list_out")
+        tab_w = held("tab_w", [P, T], I32)
+        tab_s = held("tab_s", [P, T], U8)
+        wb_w_raw = held("wb_w_raw", [P, 2 * H], U8)
+        wb_s_raw = held("wb_s_raw", [P, H], U8)
+        gain_sb = held("gain_sb", [P, GROUPS, PACK], F32)
+        wgo_sb = held("wgo_sb", [P, S], F32)
+        ident = held("ident", [P, P], F32)
+        pages = [held("page%d" % i, [P, T2], F32) for i in range(N // P)]
+
+        ap_sb = {}
+        wa_raw = {}
+        wc_raw = {}
+
+        def load_ap(c, g):
+            j0, w = CHUNKS[c]
+            ap_sb[c, g] = held("ap%d_%d" % (c, g), [P, PACK, w], F32)
+            rows = airport[g * BANK : (g + 1) * BANK, j0 : j0 + w]
+            nc.sync.dma_start(out=ap_sb[c, g][:], in_=rows.rearrange("(p t) j -> p t j", t=PACK))
+
+        def load_wa(g):
+            wa_raw[g] = held("wa_raw%d" % g, [P, PACK, BANK], F32)
+            nc.sync.dma_start(
+                out=wa_raw[g][:], in_=wa[:, g * BANK : (g + 1) * BANK].rearrange("(p i) r -> p i r", i=PACK)
+            )
+
+        def load_plane(queue, plane, rows):
+            for q in range(4):
+                queue.dma_start(
+                    out=plane[32 * q : 32 * q + 4, :].bitcast(I32), in_=rows[4 * q : 4 * q + 4, :].bitcast(I32)
+                )
+
+        def load_wc(g):
+            wc_raw[g] = held("wc_raw%d" % g, [P, PACK, N], F32)
+            nc.sync.dma_start(
+                out=wc_raw[g][:], in_=wc[g * BANK : (g + 1) * BANK, :].rearrange("(p t) n -> p t n", t=PACK)
+            )
+
+        nc.vector.memset(tab_s[:].bitcast(I32), 0)
+        nc.vector.memset(wb_s_raw[:].bitcast(I32), 0)
+        for name in HEAD.split():
+            if name == "rep":
+                nc.sync.dma_start(list_rep[:], offs2)
+            if name == "bag":
+                nc.sync.dma_start(list_bag[:], offs)
+            if name == "out":
+                nc.sync.dma_start(list_out[:], offs3)
+            if name == "ts":
+                load_plane(nc.sync, tab_s, tab_scales[0])
+            if name == "TS":
+                load_plane(nc.scalar, tab_s, tab_scales[0])
+            if name == "bs":
+                load_plane(nc.sync, wb_s_raw, wb_scales[0])
+            if name == "BS":
+                load_plane(nc.scalar, wb_s_raw, wb_scales[0])
+            if name == "gs":
+                load_plane(nc.gpsimd, wb_s_raw, wb_scales[0])
+            if name == "tw":
+                nc.sync.dma_start(out=tab_w[:], in_=tab_words[0].rearrange("p t i -> p (t i)").bitcast(I32))
+            if name == "bw":
+                nc.sync.dma_start(out=wb_w_raw[:].bitcast(I32), in_=wb_words[0].bitcast(I32))
+            if name == "gain":
+                nc.sync.dma_start(out=gain_sb[:], in_=gain.rearrange("(g p t) -> p g t", g=GROUPS, t=PACK))
+            if name == "GAIN":
+                nc.scalar.dma_start(out=gain_sb[:], in_=gain.rearrange("(g p t) -> p g t", g=GROUPS, t=PACK))
+            if name == "wgo":
+                nc.sync.dma_start(out=wgo_sb[:], in_=wgo)
+            if name.startswith("wa"):
+                load_wa(int(name[2]))
+            if name.startswith("wc"):
+                load_wc(int(name[2]))
+            if name.startswith("ap"):
+                load_ap(int(name[2]), int(name[3]))
+
+        make_identity(nc, ident[:])
+        for page in pages:
+            nc.gpsimd.memset(page[:], 0.0)
+
+        got_w = {}
+        got_s = {}
+        lists = {"rep": list_rep, "bag": list_bag}
+        cols = HALF // 16
+
+        def gather_scales(side, h):
+            got_s[side, h] = held("got_s_%s%d" % (side, h), [P, HALF], U8)
+            nc.vector.tensor_copy(got_s[side, h][:], tab_s[:].indirect(lists[side][:, h * cols : (h + 1) * cols]))
+
+        def gather_words(side, h):
+            got_w[side, h] = held("got_w_%s%d" % (side, h), [P, HALF], I32)
+            nc.vector.tensor_copy(
+                got_w[side, h][:].bitcast(U32),
+                tab_w[:].bitcast(U32).indirect(lists[side][:, h * cols : (h + 1) * cols]),
+            )
+
+        for h in range(2):
+            gather_scales("rep", h)
+            gather_scales("bag", h)
+        gather_words("rep", 0)
+        gather_words("bag", 0)
+
+        wb_w = held("wb_w", [P, 2 * H], U8)
+        wb_s = held("wb_s", [P, H], U8)
+        for g in range(GROUPS):
+            nc.vector.tensor_copy(
+                wb_w[:, 2 * g * BANK : 2 * (g + 1) * BANK].bitcast(U16).rearrange("p (t m) -> p m t", t=PACK),
+                wb_w_raw[:, 2 * g * BANK : 2 * (g + 1) * BANK].bitcast(U16).rearrange("p (m t) -> p m t", t=PACK),
+            )
+            nc.vector.tensor_copy(
+                wb_s[:, g * BANK : (g + 1) * BANK].rearrange("p (t m) -> p m t", t=PACK),
+                wb_s_raw[:, g * BANK : (g + 1) * BANK].rearrange("p (m t) -> p m t", t=PACK),
+            )
+
+        def quantise(name, grouped, width):
+            codes = held(name + "_codes", [P, width], U32)
+            scales = held(name + "_scales", [P, width], U8)
+            nc.vector.quantize_mx(out=codes[:].bitcast(FP8X4), scales=scales[:], in_=grouped)
+            return codes, scales
+
+        wa_q = {}
+        wc_q = {}
+
+        def prepare_wa(g):
+            grouped = held("wa_bf%d" % g, [P, BANK * PACK], BF16)
+            nc.scalar.copy(
+                grouped[:].rearrange("p (t m i) -> p m i t", t=PACK, i=PACK),
+                wa_raw[g][:].rearrange("p i (m t) -> p m i t", t=PACK),
+            )
+            wa_q[g] = quantise("wa%d" % g, grouped[:], BANK)
+
+        def interleave(copy, dst, src):
+            copy(
+                dst.rearrange("p (c i t) -> p c t i", i=4, t=PACK), src.rearrange("p t (c i) -> p c t i", i=4)
+            )
+
+        def prepare_wc(g):
+            grouped = held("wc_bf%d" % g, [P, N * PACK], BF16)
+            interleave(nc.vector.tensor_copy if WC_V[g] else nc.scalar.copy, grouped[:], wc_raw[g][:])
+            wc_q[g] = quantise("wc%d" % g, grouped[:], N)
+
+        units = []
+        for c, (j0, w) in enumerate(CHUNKS):
+            for g in range(GROUPS):
+                for t0 in range(0, PACK, BANK // w):
+                    units.append((c, g, t0))
+
+        def moving(side, c):
+            j0, w = CHUNKS[c]
+            h, off = divmod(j0, HALF)
+            return got_w[side, h][:, off : off + w].bitcast(FP8X4), got_s[side, h][:, off : off + w]
+
+        def ap_unit(u):
+            c, g, t0 = u
+            return ap_sb[c, g][:, t0 : t0 + BANK // CHUNKS[c][1], :].rearrange("p t j -> p (t j)")
+
+        state = {}
+
+        def stage_a(u):
+            c, g, t0 = u
+            w = CHUNKS[c][1]
+            if PE_ADD[c]:
+                acc = bank_a[units.index(u) % NA]
+            else:
+                acc = bank_turn[units.index(u) % 2]
+            rhs, rhs_scale = moving("bag", c)
+            for d in range(BANK // w):
+                m = slice((t0 + d) * P, (t0 + d + 1) * P)
+                nc.tensor.matmul_mx(
+                    out=acc[:, d * w : (d + 1) * w],
+                    lhsT=wa_q[g][0][:, m].bitcast(FP8X4),
+                    lhsT_scale=wa_q[g][1][:, m],
+                    rhs=rhs,
+                    rhs_scale=rhs_scale,
+                    start=True,
+                    stop=True,
+                )
+            staged = ring_a[units.index(u) % len(ring_a)]
+            if PE_ADD[c]:
+                nc.scalar.copy(staged[:], acc[:])
+            else:
+                nc.vector.tensor_tensor(staged[:], acc[:], ap_unit(u), ALU.add)
+            state["a", u] = staged
+
+        def stage_b(u):
+            c, g, t0 = u
+            staged = state["a", u]
+            bags = ring_bags[units.index(u) % len(ring_bags)]
+            if PE_ADD[c]:
+                turned = bank_turn[units.index(u) % 2]
+                for b in range(BANK // P):
+                    blk = slice(b * P, (b + 1) * P)
+                    nc.tensor.matmul(
+                        turned[:, blk], lhsT=ap_unit(u)[:, blk], rhs=ident[:], start=True, stop=False, is_transpose=True
+                    )
+                    nc.tensor.matmul(
+                        turned[:, blk], lhsT=staged[:, blk], rhs=ident[:], start=False, stop=True, is_transpose=True
+                    )
+                nc.scalar.activation(bags[:], turned[:], ACT.Tanh)
+            else:
+                nc.scalar.activation(bags[:], staged[:], ACT.Tanh)
+            state["t", u] = bags
+
+        def stage_r(u):
+            c, g, t0 = u
+            w = CHUNKS[c][1]
+            acc = bank_b[units.index(u) % NB]
+            rhs, rhs_scale = moving("rep", c)
+            for d in range(BANK // w):
+                m0 = g * BANK + (t0 + d) * P
+                nc.tensor.matmul_mx(
+                    out=acc[:, d * w : (d + 1) * w],
+                    lhsT=wb_w[:, 2 * m0 : 2 * (m0 + P)].bitcast(FP4X4),
+                    lhsT_scale=wb_s[:, m0 : m0 + P],
+                    rhs=rhs,
+                    rhs_scale=rhs_scale,
+                    start=True,
+                    stop=True,
+                )
+            rep = ring_rep[units.index(u) % len(ring_rep)]
+            for d in range(BANK // w):
+                blk = slice(d * w, (d + 1) * w)
+                nc.vector.scalar_tensor_tensor(
+                    rep[:, blk], acc[:, blk], gain_sb[:, g, t0 + d : t0 + d + 1], ap_unit(u)[:, blk], ALU.mult, ALU.mult
+                )
+            state["r", u] = rep
+
+        def stage_z(u):
+            c, g, t0 = u
+            w = CHUNKS[c][1]
+            bags = state["t", u]
+            if PE_ADD[c]:
+                back = bank_back[units.index(u) % NBACK]
+                for b in range(BANK // P):
+                    blk = slice(b * P, (b + 1) * P)
+                    nc.tensor.transpose(back[:, blk], bags[:, blk], ident[:])
+                bags = back
+            if t0 == 0:
+                state["z", c, g] = ring_z[g]
+            for d in range(BANK // w):
+                blk = slice(d * w, (d + 1) * w)
+                nc.vector.scalar_tensor_tensor(
+                    state["z", c, g][:, t0 + d, :],
+                    bags[:, blk],
+                    gain_sb[:, g, t0 + d : t0 + d + 1],
+                    state["r", u][:, blk],
+                    ALU.mult,
+                    ALU.subtract,
+                )
+            if t0 + BANK // w == PACK:
+                grouped = ring_zbf[g]
+                interleave(nc.scalar.copy, grouped[:], state["z", c, g][:])
+                state["zq", c, g] = quantise("z%d_%d" % (c, g), grouped[:], w)
+
+        def product(parts, acc, mag):
+            w = CHUNKS[0][1]
+            for d, (c, i) in enumerate(parts):
+                m = slice(i * P, (i + 1) * P)
+                for g in range(GROUPS):
+                    nc.tensor.matmul_mx(
+                        out=acc[:, d * w : (d + 1) * w],
+                        lhsT=wc_q[g][0][:, m].bitcast(FP8X4),
+                        lhsT_scale=wc_q[g][1][:, m],
+                        rhs=state["zq", c, g][0][:].bitcast(FP8X4),
+                        rhs_scale=state["zq", c, g][1][:],
+                        start=(g == 0),
+                        stop=(g == GROUPS - 1),
+                    )
+            nc.scalar.activation(mag, acc[:, 0 : len(parts) * w], ACT.Abs)
+
+        def place(i, j0, values):
+            w = values.shape[1]
+            nc.vector.tensor_tensor(
+                pages[i][:].indirect(list_out[:, j0 // 16 : (j0 + w) // 16]), values, wgo_sb[:, j0 : j0 + w], ALU.mult
+            )
+            if j0 + w == S:
+                nc.sync.dma_start(out=out[i * P : (i + 1) * P, :], in_=pages[i][:])
+
+        def y_bank(n):
+            if YB == "y":
+                return bank_y[0]
+            if YB == "a":
+                return bank_a[n % NA]
+            if YB == "b":
+                return bank_b[n % NB]
+            if YB == "back":
+                return bank_back[n % NBACK]
+            return bank_turn[n % 2]
+
+        count = len(units)
+        jobs = [(c, i) for c in range(2) for i in range(4)]
+        for step in range(count + 2):
+            if step < count:
+                u = units[step]
+                if u[0] == 0 and u[2] == 0:
+                    prepare_wa(u[1])
+                stage_r(u)
+                stage_a(u)
+            if step == 1:
+                gather_words("rep", 1)
+                gather_words("bag", 1)
+            if 1 <= step <= count:
+                stage_b(units[step - 1])
+            if step in (2, 3):
+                prepare_wc(step - 2)
+            if step >= 2:
+                stage_z(units[step - 2])
+                seen = 0
+                for n, (c, i) in enumerate(jobs):
+                    if JOBS[n] == step - 2:
+                        if GATE == "rep" and seen < 2:
+                            h = (GH + seen) % 2
+                            mag = ring_rep[(step - 2) % len(ring_rep)][:, h * 256 : (h + 1) * 256]
+                        else:
+                            mag = ring_mag[n % 2][:, 0:256]
+                        seen = seen + 1
+                        product([(c, i)], y_bank(step - 2 + LAG), mag)
+                        place(i, CHUNKS[c][0], mag)
+        for i in range(4):
+            mag = ring_a[i % 2] if FIN == "a" else ring_mag[i % 2]
+            product([(2, i), (3, i)], bank_turn[i % 2], mag[:])
+            place(i, CHUNKS[2][0], mag[:])

@@ -23,20 +23,26 @@ BANK = 512
 GROUPS = H // (P * PACK)
 HALF = S // 2
 CHUNKS = ((0, 256), (256, 256), (512, 256), (768, 256))
-PE_ADD = (False, True, True, True)
+PE_ADD = "vvvvpvpvpvpvpvpv"
 GATE = "rep"
 HEAD = "rep bag bw ts tw bs gain wa0 ap00 wa1 ap01 wc0 wc1 ap10 ap11 out wgo ap20 ap21 ap30 ap31"
-WC_V = (0, 1)
+WC_V = (0, 0)
 LAG = 0
 REPS = 4
-NA = 2
-NB = 1
-NBACK = 2
+NA = 1
+NB = 2
+NBACK = 1
 YB = "y"
 RA = 3
 RBAG = 4
 JOBS = (5, 7, 9, 11, 13, 15, 15, 15)
 GH = 0
+LATE = 1
+SPLIT = 1
+NT = 1
+NV = 2
+ORDER = "rabz"
+RL = 0
 FIN = "a"
 
 
@@ -48,8 +54,8 @@ def tile_list_bag_report_tracing_kernel(
         keep = ctx.enter_context(tc.tile_pool(name="keep", bufs=1))
         psum = ctx.enter_context(tc.psum_pool(name="psum", bufs=1))
 
-        def held(name, shape, dtype):
-            return keep.tile(shape, dtype, name=name, align_bytes=64)
+        def held(name, shape, dtype, tag=""):
+            return keep.tile(shape, dtype, name=name, tag=tag or name, align_bytes=64)
 
         def ring(name, count, shape, dtype):
             return [held("%s%d" % (name, i), shape, dtype) for i in range(count)]
@@ -58,7 +64,8 @@ def tile_list_bag_report_tracing_kernel(
             return [psum.tile([P, BANK], F32, name="%s%d" % (name, i)) for i in range(count)]
 
         bank_a = banks("bank_a", NA)
-        bank_turn = banks("bank_turn", 2)
+        bank_turn = banks("bank_turn", NT)
+        bank_v = banks("bank_v", NV) if NV else bank_turn
         bank_b = banks("bank_b", NB)
         bank_back = banks("bank_back", NBACK)
         bank_y = banks("bank_y", 1) if YB == "y" else None
@@ -75,7 +82,7 @@ def tile_list_bag_report_tracing_kernel(
         tab_w = held("tab_w", [P, T], I32)
         tab_s = held("tab_s", [P, T], U8)
         wb_w_raw = held("wb_w_raw", [P, 2 * H], U8)
-        wb_s_raw = held("wb_s_raw", [P, H], U8)
+        wb_s_raw = held("wb_s_raw", [P, H], U8, "late_rep")
         gain_sb = held("gain_sb", [P, GROUPS, PACK], F32)
         wgo_sb = held("wgo_sb", [P, S], F32)
         ident = held("ident", [P, P], F32)
@@ -109,7 +116,11 @@ def tile_list_bag_report_tracing_kernel(
                 out=wc_raw[g][:], in_=wc[g * BANK : (g + 1) * BANK, :].rearrange("(p t) n -> p t n", t=PACK)
             )
 
-        nc.vector.memset(tab_s[:].bitcast(I32), 0)
+        if SPLIT:
+            nc.gpsimd.memset(tab_s[:, 0 : T // 2].bitcast(I32), 0)
+            nc.vector.memset(tab_s[:, T // 2 : T].bitcast(I32), 0)
+        else:
+            nc.vector.memset(tab_s[:].bitcast(I32), 0)
         nc.vector.memset(wb_s_raw[:].bitcast(I32), 0)
         for name in HEAD.split():
             if name == "rep":
@@ -159,15 +170,15 @@ def tile_list_bag_report_tracing_kernel(
             nc.vector.tensor_copy(got_s[side, h][:], tab_s[:].indirect(lists[side][:, h * cols : (h + 1) * cols]))
 
         def gather_words(side, h):
-            got_w[side, h] = held("got_w_%s%d" % (side, h), [P, HALF], I32)
+            got_w[side, h] = held("got_w_%s%d" % (side, h), [P, HALF], I32, "late_" + side if h and LATE else "")
             nc.vector.tensor_copy(
                 got_w[side, h][:].bitcast(U32),
                 tab_w[:].bitcast(U32).indirect(lists[side][:, h * cols : (h + 1) * cols]),
             )
 
-        for h in range(2):
-            gather_scales("rep", h)
-            gather_scales("bag", h)
+        for side in ("rep", "bag"):
+            for h in range(2):
+                gather_scales(side, h)
         gather_words("rep", 0)
         gather_words("bag", 0)
 
@@ -193,7 +204,7 @@ def tile_list_bag_report_tracing_kernel(
         wc_q = {}
 
         def prepare_wa(g):
-            grouped = held("wa_bf%d" % g, [P, BANK * PACK], BF16)
+            grouped = held("wa_bf%d" % g, [P, BANK * PACK], BF16, "" if g else "late_bag")
             nc.scalar.copy(
                 grouped[:].rearrange("p (t m i) -> p m i t", t=PACK, i=PACK),
                 wa_raw[g][:].rearrange("p i (m t) -> p m i t", t=PACK),
@@ -227,13 +238,17 @@ def tile_list_bag_report_tracing_kernel(
 
         state = {}
 
+        def rank(u):
+            n = units.index(u)
+            return PE_ADD[:n].count(PE_ADD[n])
+
         def stage_a(u):
             c, g, t0 = u
             w = CHUNKS[c][1]
-            if PE_ADD[c]:
-                acc = bank_a[units.index(u) % NA]
+            if PE_ADD[units.index(u)] == "p":
+                acc = bank_a[rank(u) % NA]
             else:
-                acc = bank_turn[units.index(u) % 2]
+                acc = bank_v[(rank(u) if NV else units.index(u)) % len(bank_v)]
             rhs, rhs_scale = moving("bag", c)
             for d in range(BANK // w):
                 m = slice((t0 + d) * P, (t0 + d + 1) * P)
@@ -247,7 +262,7 @@ def tile_list_bag_report_tracing_kernel(
                     stop=True,
                 )
             staged = ring_a[units.index(u) % len(ring_a)]
-            if PE_ADD[c]:
+            if PE_ADD[units.index(u)] == "p":
                 nc.scalar.copy(staged[:], acc[:])
             else:
                 nc.vector.tensor_tensor(staged[:], acc[:], ap_unit(u), ALU.add)
@@ -257,8 +272,8 @@ def tile_list_bag_report_tracing_kernel(
             c, g, t0 = u
             staged = state["a", u]
             bags = ring_bags[units.index(u) % len(ring_bags)]
-            if PE_ADD[c]:
-                turned = bank_turn[units.index(u) % 2]
+            if PE_ADD[units.index(u)] == "p":
+                turned = bank_turn[(rank(u) if NV else units.index(u)) % NT]
                 for b in range(BANK // P):
                     blk = slice(b * P, (b + 1) * P)
                     nc.tensor.matmul(
@@ -300,8 +315,8 @@ def tile_list_bag_report_tracing_kernel(
             c, g, t0 = u
             w = CHUNKS[c][1]
             bags = state["t", u]
-            if PE_ADD[c]:
-                back = bank_back[units.index(u) % NBACK]
+            if PE_ADD[units.index(u)] == "p":
+                back = bank_back[rank(u) % NBACK]
                 for b in range(BANK // P):
                     blk = slice(b * P, (b + 1) * P)
                     nc.tensor.transpose(back[:, blk], bags[:, blk], ident[:])
@@ -361,21 +376,23 @@ def tile_list_bag_report_tracing_kernel(
         count = len(units)
         jobs = [(c, i) for c in range(2) for i in range(4)]
         for step in range(count + 2):
-            if step < count:
-                u = units[step]
-                if u[0] == 0 and u[2] == 0:
-                    prepare_wa(u[1])
-                stage_r(u)
-                stage_a(u)
+            if step < count and units[step][0] == 0 and units[step][2] == 0:
+                prepare_wa(units[step][1])
             if step == 1:
                 gather_words("rep", 1)
                 gather_words("bag", 1)
-            if 1 <= step <= count:
-                stage_b(units[step - 1])
             if step in (2, 3):
                 prepare_wc(step - 2)
+            for what in ORDER:
+                if what == "r" and 0 <= step - RL < count:
+                    stage_r(units[step - RL])
+                if what == "a" and step < count:
+                    stage_a(units[step])
+                if what == "b" and 1 <= step <= count:
+                    stage_b(units[step - 1])
+                if what == "z" and step >= 2:
+                    stage_z(units[step - 2])
             if step >= 2:
-                stage_z(units[step - 2])
                 seen = 0
                 for n, (c, i) in enumerate(jobs):
                     if JOBS[n] == step - 2:
@@ -389,5 +406,5 @@ def tile_list_bag_report_tracing_kernel(
                         place(i, CHUNKS[c][0], mag)
         for i in range(4):
             mag = ring_a[i % 2] if FIN == "a" else ring_mag[i % 2]
-            product([(2, i), (3, i)], bank_turn[i % 2], mag[:])
+            product([(2, i), (3, i)], bank_b[i % NB], mag[:])
             place(i, CHUNKS[2][0], mag[:])

@@ -20,30 +20,14 @@ ACT = mybir.ActivationFunctionType
 P = 128
 PACK = 4
 BANK = 512
-GROUPS = H // (P * PACK)
+PASS = P * PACK
+GROUPS = H // PASS
+PAGES = N // P
 HALF = S // 2
-CHUNKS = ((0, 256), (256, 256), (512, 256), (768, 256))
-PE_ADD = "vvvvpvpvpvpvpvpv"
-GATE = "rep"
-HEAD = "rep bag bw ts tw bs gain wa0 ap00 wa1 ap01 wc0 wc1 ap10 ap11 out wgo ap20 ap21 ap30 ap31"
-WC_V = (0, 0)
-LAG = 0
-REPS = 4
-NA = 1
-NB = 2
-NBACK = 1
-YB = "y"
-RA = 3
-RBAG = 4
-JOBS = (5, 7, 9, 11, 13, 15, 15, 15)
-GH = 0
-LATE = 1
-SPLIT = 1
-NT = 1
-NV = 2
-ORDER = "rabz"
-RL = 0
-FIN = "a"
+CHUNK = 256
+CHUNKS = S // CHUNK
+SLOTS = BANK // CHUNK
+UNITS_PER_CHUNK = GROUPS * PACK // SLOTS
 
 
 def tile_list_bag_report_tracing_kernel(
@@ -54,8 +38,8 @@ def tile_list_bag_report_tracing_kernel(
         keep = ctx.enter_context(tc.tile_pool(name="keep", bufs=1))
         psum = ctx.enter_context(tc.psum_pool(name="psum", bufs=1))
 
-        def held(name, shape, dtype, tag=""):
-            return keep.tile(shape, dtype, name=name, tag=tag or name, align_bytes=64)
+        def held(name, shape, dtype, shares=None):
+            return keep.tile(shape, dtype, name=name, tag=shares or name, align_bytes=64)
 
         def ring(name, count, shape, dtype):
             return [held("%s%d" % (name, i), shape, dtype) for i in range(count)]
@@ -63,348 +47,278 @@ def tile_list_bag_report_tracing_kernel(
         def banks(name, count):
             return [psum.tile([P, BANK], F32, name="%s%d" % (name, i)) for i in range(count)]
 
-        bank_a = banks("bank_a", NA)
-        bank_turn = banks("bank_turn", NT)
-        bank_v = banks("bank_v", NV) if NV else bank_turn
-        bank_b = banks("bank_b", NB)
-        bank_back = banks("bank_back", NBACK)
-        bank_y = banks("bank_y", 1) if YB == "y" else None
-        ring_a = ring("a_sb", RA, [P, BANK], F32)
-        ring_bags = ring("bags", RBAG, [P, BANK], F32)
-        ring_rep = ring("rep", REPS, [P, BANK], F32)
-        ring_mag = ring("mag", 2, [P, BANK], F32)
-        ring_z = ring("z_rows", 2, [P, PACK, 256], BF16)
-        ring_zbf = ring("z_bf", 2, [P, PACK * 256], BF16)
+        bank_bag_tensor = banks("bank_bag_tensor", 1)
+        bank_turned = banks("bank_turned", 1)
+        bank_bag_vector = banks("bank_bag_vector", 2)
+        bank_report = banks("bank_report", 2)
+        bank_back = banks("bank_back", 1)
+        bank_y = banks("bank_y", 1)
+        ring_staged = ring("staged", 3, [P, BANK], F32)
+        ring_bags = ring("bags", 4, [P, BANK], F32)
+        ring_reports = ring("reports", 4, [P, BANK], F32)
+        spare_magnitude = held("spare_magnitude", [P, CHUNK], F32)
+        ring_z_slots = ring("z_slots", GROUPS, [P, PACK, CHUNK], BF16)
+        ring_z_words = ring("z_words", GROUPS, [P, CHUNK * PACK], BF16)
 
         list_bag = keep.tile([P, S // 16], U16, name="list_bag")
-        list_rep = keep.tile([P, S // 16], U16, name="list_rep")
+        list_report = keep.tile([P, S // 16], U16, name="list_report")
         list_out = keep.tile([P, S // 16], U16, name="list_out")
+        lists = {"report": list_report, "bag": list_bag}
         tab_w = held("tab_w", [P, T], I32)
         tab_s = held("tab_s", [P, T], U8)
         wb_w_raw = held("wb_w_raw", [P, 2 * H], U8)
-        wb_s_raw = held("wb_s_raw", [P, H], U8, "late_rep")
+        wb_s_raw = held("wb_s_raw", [P, H], U8, shares="late_report")
         gain_sb = held("gain_sb", [P, GROUPS, PACK], F32)
         wgo_sb = held("wgo_sb", [P, S], F32)
         ident = held("ident", [P, P], F32)
-        pages = [held("page%d" % i, [P, T2], F32) for i in range(N // P)]
+        pages = ring("page", PAGES, [P, T2], F32)
+        wa_raw = ring("wa_raw", GROUPS, [P, PACK, PASS], F32)
+        wc_raw = ring("wc_raw", GROUPS, [P, PACK, N], F32)
+        airport_sb = [ring("airport%d_" % c, GROUPS, [P, PACK, CHUNK], F32) for c in range(CHUNKS)]
 
-        ap_sb = {}
-        wa_raw = {}
-        wc_raw = {}
+        def group_rows(g):
+            return slice(g * PASS, (g + 1) * PASS)
 
-        def load_ap(c, g):
-            j0, w = CHUNKS[c]
-            ap_sb[c, g] = held("ap%d_%d" % (c, g), [P, PACK, w], F32)
-            rows = airport[g * BANK : (g + 1) * BANK, j0 : j0 + w]
-            nc.sync.dma_start(out=ap_sb[c, g][:], in_=rows.rearrange("(p t) j -> p t j", t=PACK))
-
-        def load_wa(g):
-            wa_raw[g] = held("wa_raw%d" % g, [P, PACK, BANK], F32)
-            nc.sync.dma_start(
-                out=wa_raw[g][:], in_=wa[:, g * BANK : (g + 1) * BANK].rearrange("(p i) r -> p i r", i=PACK)
-            )
-
-        def load_plane(queue, plane, rows):
-            for q in range(4):
-                queue.dma_start(
-                    out=plane[32 * q : 32 * q + 4, :].bitcast(I32), in_=rows[4 * q : 4 * q + 4, :].bitcast(I32)
+        def load_scales(tile, rows):
+            for quad in range(4):
+                nc.sync.dma_start(
+                    out=tile[32 * quad : 32 * quad + 4, :].bitcast(I32),
+                    in_=rows[4 * quad : 4 * quad + 4, :].bitcast(I32),
                 )
 
-        def load_wc(g):
-            wc_raw[g] = held("wc_raw%d" % g, [P, PACK, N], F32)
-            nc.sync.dma_start(
-                out=wc_raw[g][:], in_=wc[g * BANK : (g + 1) * BANK, :].rearrange("(p t) n -> p t n", t=PACK)
-            )
+        def load_airport(c, g):
+            part = airport[group_rows(g), c * CHUNK : (c + 1) * CHUNK]
+            nc.sync.dma_start(out=airport_sb[c][g][:], in_=part.rearrange("(p t) j -> p t j", t=PACK))
 
-        if SPLIT:
-            nc.gpsimd.memset(tab_s[:, 0 : T // 2].bitcast(I32), 0)
-            nc.vector.memset(tab_s[:, T // 2 : T].bitcast(I32), 0)
-        else:
-            nc.vector.memset(tab_s[:].bitcast(I32), 0)
+        nc.gpsimd.memset(tab_s[:, 0 : T // 2].bitcast(I32), 0)
+        nc.vector.memset(tab_s[:, T // 2 : T].bitcast(I32), 0)
         nc.vector.memset(wb_s_raw[:].bitcast(I32), 0)
-        for name in HEAD.split():
-            if name == "rep":
-                nc.sync.dma_start(list_rep[:], offs2)
-            if name == "bag":
-                nc.sync.dma_start(list_bag[:], offs)
-            if name == "out":
-                nc.sync.dma_start(list_out[:], offs3)
-            if name == "ts":
-                load_plane(nc.sync, tab_s, tab_scales[0])
-            if name == "TS":
-                load_plane(nc.scalar, tab_s, tab_scales[0])
-            if name == "bs":
-                load_plane(nc.sync, wb_s_raw, wb_scales[0])
-            if name == "BS":
-                load_plane(nc.scalar, wb_s_raw, wb_scales[0])
-            if name == "gs":
-                load_plane(nc.gpsimd, wb_s_raw, wb_scales[0])
-            if name == "tw":
-                nc.sync.dma_start(out=tab_w[:], in_=tab_words[0].rearrange("p t i -> p (t i)").bitcast(I32))
-            if name == "bw":
-                nc.sync.dma_start(out=wb_w_raw[:].bitcast(I32), in_=wb_words[0].bitcast(I32))
-            if name == "gain":
-                nc.sync.dma_start(out=gain_sb[:], in_=gain.rearrange("(g p t) -> p g t", g=GROUPS, t=PACK))
-            if name == "GAIN":
-                nc.scalar.dma_start(out=gain_sb[:], in_=gain.rearrange("(g p t) -> p g t", g=GROUPS, t=PACK))
-            if name == "wgo":
-                nc.sync.dma_start(out=wgo_sb[:], in_=wgo)
-            if name.startswith("wa"):
-                load_wa(int(name[2]))
-            if name.startswith("wc"):
-                load_wc(int(name[2]))
-            if name.startswith("ap"):
-                load_ap(int(name[2]), int(name[3]))
+
+        nc.sync.dma_start(list_report[:], offs2)
+        nc.sync.dma_start(list_bag[:], offs)
+        nc.sync.dma_start(out=wb_w_raw[:].bitcast(I32), in_=wb_words[0].bitcast(I32))
+        load_scales(tab_s, tab_scales[0])
+        nc.sync.dma_start(out=tab_w[:], in_=tab_words[0].rearrange("p t i -> p (t i)").bitcast(I32))
+        load_scales(wb_s_raw, wb_scales[0])
+        nc.sync.dma_start(out=gain_sb[:], in_=gain.rearrange("(g p t) -> p g t", g=GROUPS, t=PACK))
+        for g in range(GROUPS):
+            nc.sync.dma_start(out=wa_raw[g][:], in_=wa[:, group_rows(g)].rearrange("(p i) r -> p i r", i=PACK))
+            load_airport(0, g)
+        for g in range(GROUPS):
+            nc.sync.dma_start(out=wc_raw[g][:], in_=wc[group_rows(g), :].rearrange("(p t) n -> p t n", t=PACK))
+        for g in range(GROUPS):
+            load_airport(1, g)
+        nc.sync.dma_start(list_out[:], offs3)
+        nc.sync.dma_start(out=wgo_sb[:], in_=wgo)
+        for c in range(2, CHUNKS):
+            for g in range(GROUPS):
+                load_airport(c, g)
 
         make_identity(nc, ident[:])
         for page in pages:
             nc.gpsimd.memset(page[:], 0.0)
 
-        got_w = {}
-        got_s = {}
-        lists = {"rep": list_rep, "bag": list_bag}
-        cols = HALF // 16
+        got_words = {}
+        got_scales = {}
 
-        def gather_scales(side, h):
-            got_s[side, h] = held("got_s_%s%d" % (side, h), [P, HALF], U8)
-            nc.vector.tensor_copy(got_s[side, h][:], tab_s[:].indirect(lists[side][:, h * cols : (h + 1) * cols]))
+        def entries(offsets, start, width):
+            return offsets[:, start // 16 : (start + width) // 16]
 
-        def gather_words(side, h):
-            got_w[side, h] = held("got_w_%s%d" % (side, h), [P, HALF], I32, "late_" + side if h and LATE else "")
-            nc.vector.tensor_copy(
-                got_w[side, h][:].bitcast(U32),
-                tab_w[:].bitcast(U32).indirect(lists[side][:, h * cols : (h + 1) * cols]),
-            )
+        def gather_words(side, half, shares=None):
+            tile = held("got_words_%s%d" % (side, half), [P, HALF], I32, shares)
+            offsets = entries(lists[side], half * HALF, HALF)
+            nc.vector.tensor_copy(tile[:].bitcast(U32), tab_w[:].bitcast(U32).indirect(offsets))
+            got_words[side, half] = tile
 
-        for side in ("rep", "bag"):
-            for h in range(2):
-                gather_scales(side, h)
-        gather_words("rep", 0)
-        gather_words("bag", 0)
+        for side in lists:
+            for half in range(2):
+                got_scales[side, half] = held("got_scales_%s%d" % (side, half), [P, HALF], U8)
+                offsets = entries(lists[side], half * HALF, HALF)
+                nc.vector.tensor_copy(got_scales[side, half][:], tab_s[:].indirect(offsets))
+        for side in lists:
+            gather_words(side, 0)
 
         wb_w = held("wb_w", [P, 2 * H], U8)
         wb_s = held("wb_s", [P, H], U8)
         for g in range(GROUPS):
+            word_cols = slice(2 * g * PASS, 2 * (g + 1) * PASS)
             nc.vector.tensor_copy(
-                wb_w[:, 2 * g * BANK : 2 * (g + 1) * BANK].bitcast(U16).rearrange("p (t m) -> p m t", t=PACK),
-                wb_w_raw[:, 2 * g * BANK : 2 * (g + 1) * BANK].bitcast(U16).rearrange("p (m t) -> p m t", t=PACK),
+                wb_w[:, word_cols].bitcast(U16).rearrange("p (t m) -> p m t", t=PACK),
+                wb_w_raw[:, word_cols].bitcast(U16).rearrange("p (m t) -> p m t", t=PACK),
             )
             nc.vector.tensor_copy(
-                wb_s[:, g * BANK : (g + 1) * BANK].rearrange("p (t m) -> p m t", t=PACK),
-                wb_s_raw[:, g * BANK : (g + 1) * BANK].rearrange("p (m t) -> p m t", t=PACK),
+                wb_s[:, group_rows(g)].rearrange("p (t m) -> p m t", t=PACK),
+                wb_s_raw[:, group_rows(g)].rearrange("p (m t) -> p m t", t=PACK),
             )
 
-        def quantise(name, grouped, width):
+        def quantise(name, values, width):
             codes = held(name + "_codes", [P, width], U32)
             scales = held(name + "_scales", [P, width], U8)
-            nc.vector.quantize_mx(out=codes[:].bitcast(FP8X4), scales=scales[:], in_=grouped)
+            nc.vector.quantize_mx(out=codes[:].bitcast(FP8X4), scales=scales[:], in_=values)
             return codes, scales
 
-        wa_q = {}
-        wc_q = {}
-
-        def prepare_wa(g):
-            grouped = held("wa_bf%d" % g, [P, BANK * PACK], BF16, "" if g else "late_bag")
+        def interleave(dst, src):
             nc.scalar.copy(
-                grouped[:].rearrange("p (t m i) -> p m i t", t=PACK, i=PACK),
-                wa_raw[g][:].rearrange("p i (m t) -> p m i t", t=PACK),
-            )
-            wa_q[g] = quantise("wa%d" % g, grouped[:], BANK)
-
-        def interleave(copy, dst, src):
-            copy(
                 dst.rearrange("p (c i t) -> p c t i", i=4, t=PACK), src.rearrange("p t (c i) -> p c t i", i=4)
             )
 
+        wa_q = {}
+        wc_q = {}
+        z_q = {}
+
+        def prepare_wa(g):
+            rounded = held("wa_bf%d" % g, [P, PASS * PACK], BF16, "late_bag" if g == 0 else None)
+            nc.scalar.copy(
+                rounded[:].rearrange("p (t m i) -> p m i t", t=PACK, i=PACK),
+                wa_raw[g][:].rearrange("p i (m t) -> p m i t", t=PACK),
+            )
+            wa_q[g] = quantise("wa%d" % g, rounded[:], PASS)
+
         def prepare_wc(g):
-            grouped = held("wc_bf%d" % g, [P, N * PACK], BF16)
-            interleave(nc.vector.tensor_copy if WC_V[g] else nc.scalar.copy, grouped[:], wc_raw[g][:])
-            wc_q[g] = quantise("wc%d" % g, grouped[:], N)
+            rounded = held("wc_bf%d" % g, [P, N * PACK], BF16)
+            interleave(rounded[:], wc_raw[g][:])
+            wc_q[g] = quantise("wc%d" % g, rounded[:], N)
 
-        units = []
-        for c, (j0, w) in enumerate(CHUNKS):
-            for g in range(GROUPS):
-                for t0 in range(0, PACK, BANK // w):
-                    units.append((c, g, t0))
+        units = [(c, g, t0) for c in range(CHUNKS) for g in range(GROUPS) for t0 in range(0, PACK, SLOTS)]
 
-        def moving(side, c):
-            j0, w = CHUNKS[c]
-            h, off = divmod(j0, HALF)
-            return got_w[side, h][:, off : off + w].bitcast(FP8X4), got_s[side, h][:, off : off + w]
+        def adds_on_tensor(n):
+            return n >= UNITS_PER_CHUNK and n % 2 == 0
 
-        def ap_unit(u):
-            c, g, t0 = u
-            return ap_sb[c, g][:, t0 : t0 + BANK // CHUNKS[c][1], :].rearrange("p t j -> p (t j)")
+        def turn(n, tiles):
+            rank = len([m for m in range(n) if adds_on_tensor(m) == adds_on_tensor(n)])
+            return tiles[rank % len(tiles)]
 
-        state = {}
+        def airport_of(n):
+            c, g, t0 = units[n]
+            return airport_sb[c][g][:, t0 : t0 + SLOTS, :].rearrange("p t j -> p (t j)")
 
-        def rank(u):
-            n = units.index(u)
-            return PE_ADD[:n].count(PE_ADD[n])
-
-        def stage_a(u):
-            c, g, t0 = u
-            w = CHUNKS[c][1]
-            if PE_ADD[units.index(u)] == "p":
-                acc = bank_a[rank(u) % NA]
-            else:
-                acc = bank_v[(rank(u) if NV else units.index(u)) % len(bank_v)]
-            rhs, rhs_scale = moving("bag", c)
-            for d in range(BANK // w):
-                m = slice((t0 + d) * P, (t0 + d + 1) * P)
+        def first_product(n, side, acc):
+            c, g, t0 = units[n]
+            half, first = divmod(c * CHUNK, HALF)
+            for d in range(SLOTS):
+                col = (t0 + d) * P
+                if side == "bag":
+                    weights = wa_q[g][0][:, col : col + P].bitcast(FP8X4)
+                    weight_scales = wa_q[g][1][:, col : col + P]
+                else:
+                    col = g * PASS + col
+                    weights = wb_w[:, 2 * col : 2 * (col + P)].bitcast(FP4X4)
+                    weight_scales = wb_s[:, col : col + P]
                 nc.tensor.matmul_mx(
-                    out=acc[:, d * w : (d + 1) * w],
-                    lhsT=wa_q[g][0][:, m].bitcast(FP8X4),
-                    lhsT_scale=wa_q[g][1][:, m],
-                    rhs=rhs,
-                    rhs_scale=rhs_scale,
+                    out=acc[:, d * CHUNK : (d + 1) * CHUNK],
+                    lhsT=weights,
+                    lhsT_scale=weight_scales,
+                    rhs=got_words[side, half][:, first : first + CHUNK].bitcast(FP8X4),
+                    rhs_scale=got_scales[side, half][:, first : first + CHUNK],
                     start=True,
                     stop=True,
                 )
-            staged = ring_a[units.index(u) % len(ring_a)]
-            if PE_ADD[units.index(u)] == "p":
+
+        def scale_and_combine(n, dst, src, other, op):
+            c, g, t0 = units[n]
+            for d in range(SLOTS):
+                cols = slice(d * CHUNK, (d + 1) * CHUNK)
+                nc.vector.scalar_tensor_tensor(
+                    dst[:, cols], src[:, cols], gain_sb[:, g, t0 + d : t0 + d + 1], other[:, cols], ALU.mult, op
+                )
+
+        def stage_reports(n):
+            acc = bank_report[n % len(bank_report)]
+            first_product(n, "report", acc)
+            scale_and_combine(n, ring_reports[n % len(ring_reports)], acc, airport_of(n), ALU.mult)
+
+        def stage_bag_product(n):
+            staged = ring_staged[n % len(ring_staged)]
+            acc = turn(n, bank_bag_tensor if adds_on_tensor(n) else bank_bag_vector)
+            first_product(n, "bag", acc)
+            if adds_on_tensor(n):
                 nc.scalar.copy(staged[:], acc[:])
             else:
-                nc.vector.tensor_tensor(staged[:], acc[:], ap_unit(u), ALU.add)
-            state["a", u] = staged
+                nc.vector.tensor_tensor(staged[:], acc[:], airport_of(n), ALU.add)
 
-        def stage_b(u):
-            c, g, t0 = u
-            staged = state["a", u]
-            bags = ring_bags[units.index(u) % len(ring_bags)]
-            if PE_ADD[units.index(u)] == "p":
-                turned = bank_turn[(rank(u) if NV else units.index(u)) % NT]
-                for b in range(BANK // P):
-                    blk = slice(b * P, (b + 1) * P)
-                    nc.tensor.matmul(
-                        turned[:, blk], lhsT=ap_unit(u)[:, blk], rhs=ident[:], start=True, stop=False, is_transpose=True
-                    )
-                    nc.tensor.matmul(
-                        turned[:, blk], lhsT=staged[:, blk], rhs=ident[:], start=False, stop=True, is_transpose=True
-                    )
-                nc.scalar.activation(bags[:], turned[:], ACT.Tanh)
-            else:
-                nc.scalar.activation(bags[:], staged[:], ACT.Tanh)
-            state["t", u] = bags
+        def stage_tanh(n):
+            total = ring_staged[n % len(ring_staged)]
+            if adds_on_tensor(n):
+                turned = turn(n, bank_turned)
+                for first in range(0, BANK, P):
+                    cols = slice(first, first + P)
+                    for term, opens in ((airport_of(n), True), (total, False)):
+                        nc.tensor.matmul(
+                            turned[:, cols],
+                            lhsT=term[:, cols],
+                            rhs=ident[:],
+                            start=opens,
+                            stop=not opens,
+                            is_transpose=True,
+                        )
+                total = turned
+            nc.scalar.activation(ring_bags[n % len(ring_bags)][:], total[:], ACT.Tanh)
 
-        def stage_r(u):
-            c, g, t0 = u
-            w = CHUNKS[c][1]
-            acc = bank_b[units.index(u) % NB]
-            rhs, rhs_scale = moving("rep", c)
-            for d in range(BANK // w):
-                m0 = g * BANK + (t0 + d) * P
-                nc.tensor.matmul_mx(
-                    out=acc[:, d * w : (d + 1) * w],
-                    lhsT=wb_w[:, 2 * m0 : 2 * (m0 + P)].bitcast(FP4X4),
-                    lhsT_scale=wb_s[:, m0 : m0 + P],
-                    rhs=rhs,
-                    rhs_scale=rhs_scale,
-                    start=True,
-                    stop=True,
-                )
-            rep = ring_rep[units.index(u) % len(ring_rep)]
-            for d in range(BANK // w):
-                blk = slice(d * w, (d + 1) * w)
-                nc.vector.scalar_tensor_tensor(
-                    rep[:, blk], acc[:, blk], gain_sb[:, g, t0 + d : t0 + d + 1], ap_unit(u)[:, blk], ALU.mult, ALU.mult
-                )
-            state["r", u] = rep
-
-        def stage_z(u):
-            c, g, t0 = u
-            w = CHUNKS[c][1]
-            bags = state["t", u]
-            if PE_ADD[units.index(u)] == "p":
-                back = bank_back[rank(u) % NBACK]
-                for b in range(BANK // P):
-                    blk = slice(b * P, (b + 1) * P)
-                    nc.tensor.transpose(back[:, blk], bags[:, blk], ident[:])
+        def stage_z(n):
+            c, g, t0 = units[n]
+            bags = ring_bags[n % len(ring_bags)]
+            if adds_on_tensor(n):
+                back = turn(n, bank_back)
+                for first in range(0, BANK, P):
+                    nc.tensor.transpose(back[:, first : first + P], bags[:, first : first + P], ident[:])
                 bags = back
-            if t0 == 0:
-                state["z", c, g] = ring_z[g]
-            for d in range(BANK // w):
-                blk = slice(d * w, (d + 1) * w)
-                nc.vector.scalar_tensor_tensor(
-                    state["z", c, g][:, t0 + d, :],
-                    bags[:, blk],
-                    gain_sb[:, g, t0 + d : t0 + d + 1],
-                    state["r", u][:, blk],
-                    ALU.mult,
-                    ALU.subtract,
-                )
-            if t0 + BANK // w == PACK:
-                grouped = ring_zbf[g]
-                interleave(nc.scalar.copy, grouped[:], state["z", c, g][:])
-                state["zq", c, g] = quantise("z%d_%d" % (c, g), grouped[:], w)
+            z_unit = ring_z_slots[g][:, t0 : t0 + SLOTS, :].rearrange("p t j -> p (t j)")
+            scale_and_combine(n, z_unit, bags, ring_reports[n % len(ring_reports)], ALU.subtract)
 
-        def product(parts, acc, mag):
-            w = CHUNKS[0][1]
-            for d, (c, i) in enumerate(parts):
-                m = slice(i * P, (i + 1) * P)
+        def quantise_z(c, g):
+            interleave(ring_z_words[g][:], ring_z_slots[g][:])
+            z_q[c, g] = quantise("z%d_%d" % (c, g), ring_z_words[g][:], CHUNK)
+
+        def place(page, chunks, acc, magnitude):
+            rows = slice(page * P, (page + 1) * P)
+            for d, c in enumerate(chunks):
                 for g in range(GROUPS):
                     nc.tensor.matmul_mx(
-                        out=acc[:, d * w : (d + 1) * w],
-                        lhsT=wc_q[g][0][:, m].bitcast(FP8X4),
-                        lhsT_scale=wc_q[g][1][:, m],
-                        rhs=state["zq", c, g][0][:].bitcast(FP8X4),
-                        rhs_scale=state["zq", c, g][1][:],
+                        out=acc[:, d * CHUNK : (d + 1) * CHUNK],
+                        lhsT=wc_q[g][0][:, rows].bitcast(FP8X4),
+                        lhsT_scale=wc_q[g][1][:, rows],
+                        rhs=z_q[c, g][0][:].bitcast(FP8X4),
+                        rhs_scale=z_q[c, g][1][:],
                         start=(g == 0),
                         stop=(g == GROUPS - 1),
                     )
-            nc.scalar.activation(mag, acc[:, 0 : len(parts) * w], ACT.Abs)
+            start, width = chunks[0] * CHUNK, len(chunks) * CHUNK
+            nc.scalar.activation(magnitude, acc[:, 0:width], ACT.Abs)
+            window = pages[page][:].indirect(entries(list_out, start, width))
+            nc.vector.tensor_tensor(window, magnitude, wgo_sb[:, start : start + width], ALU.mult)
 
-        def place(i, j0, values):
-            w = values.shape[1]
-            nc.vector.tensor_tensor(
-                pages[i][:].indirect(list_out[:, j0 // 16 : (j0 + w) // 16]), values, wgo_sb[:, j0 : j0 + w], ALU.mult
-            )
-            if j0 + w == S:
-                nc.sync.dma_start(out=out[i * P : (i + 1) * P, :], in_=pages[i][:])
-
-        def y_bank(n):
-            if YB == "y":
-                return bank_y[0]
-            if YB == "a":
-                return bank_a[n % NA]
-            if YB == "b":
-                return bank_b[n % NB]
-            if YB == "back":
-                return bank_back[n % NBACK]
-            return bank_turn[n % 2]
+        early = [(page, c) for c in range(CHUNKS // 2) for page in range(PAGES)]
 
         count = len(units)
-        jobs = [(c, i) for c in range(2) for i in range(4)]
         for step in range(count + 2):
-            if step < count and units[step][0] == 0 and units[step][2] == 0:
+            if step < UNITS_PER_CHUNK and units[step][2] == 0:
                 prepare_wa(units[step][1])
             if step == 1:
-                gather_words("rep", 1)
-                gather_words("bag", 1)
-            if step in (2, 3):
+                for side in lists:
+                    gather_words(side, 1, shares="late_" + side)
+            if 2 <= step < 2 + GROUPS:
                 prepare_wc(step - 2)
-            for what in ORDER:
-                if what == "r" and 0 <= step - RL < count:
-                    stage_r(units[step - RL])
-                if what == "a" and step < count:
-                    stage_a(units[step])
-                if what == "b" and 1 <= step <= count:
-                    stage_b(units[step - 1])
-                if what == "z" and step >= 2:
-                    stage_z(units[step - 2])
+            if step < count:
+                stage_reports(step)
+                stage_bag_product(step)
+            if 1 <= step <= count:
+                stage_tanh(step - 1)
             if step >= 2:
-                seen = 0
-                for n, (c, i) in enumerate(jobs):
-                    if JOBS[n] == step - 2:
-                        if GATE == "rep" and seen < 2:
-                            h = (GH + seen) % 2
-                            mag = ring_rep[(step - 2) % len(ring_rep)][:, h * 256 : (h + 1) * 256]
-                        else:
-                            mag = ring_mag[n % 2][:, 0:256]
-                        seen = seen + 1
-                        product([(c, i)], y_bank(step - 2 + LAG), mag)
-                        place(i, CHUNKS[c][0], mag)
-        for i in range(4):
-            mag = ring_a[i % 2] if FIN == "a" else ring_mag[i % 2]
-            product([(2, i), (3, i)], bank_b[i % NB], mag[:])
-            place(i, CHUNKS[2][0], mag[:])
+                n = step - 2
+                c, g, t0 = units[n]
+                stage_z(n)
+                if t0 + SLOTS == PACK:
+                    quantise_z(c, g)
+                    if c > 0:
+                        freed = ring_reports[n % len(ring_reports)]
+                        spaces = [freed[:, 0:CHUNK]]
+                        if n == count - 1:
+                            spaces.extend([freed[:, CHUNK:BANK], spare_magnitude[:]])
+                        for space in spaces:
+                            page, chunk = early[0]
+                            early.remove(early[0])
+                            place(page, [chunk], bank_y[0], space)
+
+        for page in range(PAGES):
+            place(page, range(CHUNKS // 2, CHUNKS), bank_report[page % 2], ring_staged[page % 2][:])
+            nc.sync.dma_start(out=out[page * P : (page + 1) * P, :], in_=pages[page][:])

from contextlib import ExitStack

import concourse.mybir as mybir
from concourse.masks import make_identity

K, H, N, T, S, T2 = 512, 1024, 512, 4096, 1024, 2048
FLOPS = 2 * (2 * K * H * S + H * N * S)

F32 = mybir.dt.float32
BF16 = mybir.dt.bfloat16
I32 = mybir.dt.int32
U32 = mybir.dt.uint32
U16 = mybir.dt.uint16
U8 = mybir.dt.uint8
FP8X4 = mybir.dt.float8_e4m3fn_x4
FP4X4 = mybir.dt.float4_e2m1fn_x4
ALU = mybir.AluOpType
ACT = mybir.ActivationFunctionType

P = 128
PACK = 4
BANK = 512
PASS = P * PACK
GROUPS = H // PASS
PAGES = N // P
HALF = S // 2
CHUNK = 256
CHUNKS = S // CHUNK
SLOTS = BANK // CHUNK
UNITS_PER_CHUNK = GROUPS * PACK // SLOTS


def tile_list_bag_report_tracing_kernel(
    tc, tab_words, tab_scales, offs, offs2, offs3, wa, wb_words, wb_scales, airport, gain, wc, wgo, out
):
    nc = tc.nc
    with ExitStack() as ctx:
        keep = ctx.enter_context(tc.tile_pool(name="keep", bufs=1))
        psum = ctx.enter_context(tc.psum_pool(name="psum", bufs=1))

        def held(name, shape, dtype, shares=None):
            return keep.tile(shape, dtype, name=name, tag=shares or name, align_bytes=64)

        def ring(name, count, shape, dtype):
            return [held("%s%d" % (name, i), shape, dtype) for i in range(count)]

        def banks(name, count):
            return [psum.tile([P, BANK], F32, name="%s%d" % (name, i)) for i in range(count)]

        bank_bag_tensor = banks("bank_bag_tensor", 1)
        bank_turned = banks("bank_turned", 1)
        bank_bag_vector = banks("bank_bag_vector", 2)
        bank_report = banks("bank_report", 2)
        bank_back = banks("bank_back", 1)
        bank_y = banks("bank_y", 1)
        ring_staged = ring("staged", 3, [P, BANK], F32)
        ring_bags = ring("bags", 4, [P, BANK], F32)
        ring_reports = ring("reports", 4, [P, BANK], F32)
        spare_magnitude = held("spare_magnitude", [P, CHUNK], F32)
        ring_z_slots = ring("z_slots", GROUPS, [P, PACK, CHUNK], BF16)
        ring_z_words = ring("z_words", GROUPS, [P, CHUNK * PACK], BF16)

        list_bag = keep.tile([P, S // 16], U16, name="list_bag")
        list_report = keep.tile([P, S // 16], U16, name="list_report")
        list_out = keep.tile([P, S // 16], U16, name="list_out")
        lists = {"report": list_report, "bag": list_bag}
        tab_w = held("tab_w", [P, T], I32)
        tab_s = held("tab_s", [P, T], U8)
        wb_w_raw = held("wb_w_raw", [P, 2 * H], U8)
        wb_s_raw = held("wb_s_raw", [P, H], U8, shares="late_report")
        gain_sb = held("gain_sb", [P, GROUPS, PACK], F32)
        wgo_sb = held("wgo_sb", [P, S], F32)
        ident = held("ident", [P, P], F32)
        pages = ring("page", PAGES, [P, T2], F32)
        wa_raw = ring("wa_raw", GROUPS, [P, PACK, PASS], F32)
        wc_raw = ring("wc_raw", GROUPS, [P, PACK, N], F32)
        airport_sb = [ring("airport%d_" % c, GROUPS, [P, PACK, CHUNK], F32) for c in range(CHUNKS)]

        def group_rows(g):
            return slice(g * PASS, (g + 1) * PASS)

        def load_scales(tile, rows):
            for quad in range(4):
                nc.sync.dma_start(
                    out=tile[32 * quad : 32 * quad + 4, :].bitcast(I32),
                    in_=rows[4 * quad : 4 * quad + 4, :].bitcast(I32),
                )

        def load_airport(c, g):
            part = airport[group_rows(g), c * CHUNK : (c + 1) * CHUNK]
            nc.sync.dma_start(out=airport_sb[c][g][:], in_=part.rearrange("(p t) j -> p t j", t=PACK))

        nc.gpsimd.memset(tab_s[:, 0 : T // 2].bitcast(I32), 0)
        nc.vector.memset(tab_s[:, T // 2 : T].bitcast(I32), 0)
        nc.vector.memset(wb_s_raw[:].bitcast(I32), 0)

        nc.sync.dma_start(list_report[:], offs2)
        nc.sync.dma_start(list_bag[:], offs)
        nc.sync.dma_start(out=wb_w_raw[:].bitcast(I32), in_=wb_words[0].bitcast(I32))
        load_scales(tab_s, tab_scales[0])
        nc.sync.dma_start(out=tab_w[:], in_=tab_words[0].rearrange("p t i -> p (t i)").bitcast(I32))
        load_scales(wb_s_raw, wb_scales[0])
        nc.sync.dma_start(out=gain_sb[:], in_=gain.rearrange("(g p t) -> p g t", g=GROUPS, t=PACK))
        for g in range(GROUPS):
            nc.sync.dma_start(out=wa_raw[g][:], in_=wa[:, group_rows(g)].rearrange("(p i) r -> p i r", i=PACK))
            load_airport(0, g)
        for g in range(GROUPS):
            nc.sync.dma_start(out=wc_raw[g][:], in_=wc[group_rows(g), :].rearrange("(p t) n -> p t n", t=PACK))
        for g in range(GROUPS):
            load_airport(1, g)
        nc.sync.dma_start(list_out[:], offs3)
        nc.sync.dma_start(out=wgo_sb[:], in_=wgo)
        for c in range(2, CHUNKS):
            for g in range(GROUPS):
                load_airport(c, g)

        make_identity(nc, ident[:])
        for page in pages:
            nc.gpsimd.memset(page[:], 0.0)

        got_words = {}
        got_scales = {}

        def entries(offsets, start, width):
            return offsets[:, start // 16 : (start + width) // 16]

        def gather_words(side, half, shares=None):
            tile = held("got_words_%s%d" % (side, half), [P, HALF], I32, shares)
            offsets = entries(lists[side], half * HALF, HALF)
            nc.vector.tensor_copy(tile[:].bitcast(U32), tab_w[:].bitcast(U32).indirect(offsets))
            got_words[side, half] = tile

        for side in lists:
            for half in range(2):
                got_scales[side, half] = held("got_scales_%s%d" % (side, half), [P, HALF], U8)
                offsets = entries(lists[side], half * HALF, HALF)
                nc.vector.tensor_copy(got_scales[side, half][:], tab_s[:].indirect(offsets))
        for side in lists:
            gather_words(side, 0)

        wb_w = held("wb_w", [P, 2 * H], U8)
        wb_s = held("wb_s", [P, H], U8)
        for g in range(GROUPS):
            word_cols = slice(2 * g * PASS, 2 * (g + 1) * PASS)
            nc.vector.tensor_copy(
                wb_w[:, word_cols].bitcast(U16).rearrange("p (t m) -> p m t", t=PACK),
                wb_w_raw[:, word_cols].bitcast(U16).rearrange("p (m t) -> p m t", t=PACK),
            )
            nc.vector.tensor_copy(
                wb_s[:, group_rows(g)].rearrange("p (t m) -> p m t", t=PACK),
                wb_s_raw[:, group_rows(g)].rearrange("p (m t) -> p m t", t=PACK),
            )

        def quantise(name, values, width):
            codes = held(name + "_codes", [P, width], U32)
            scales = held(name + "_scales", [P, width], U8)
            nc.vector.quantize_mx(out=codes[:].bitcast(FP8X4), scales=scales[:], in_=values)
            return codes, scales

        def interleave(dst, src):
            nc.scalar.copy(
                dst.rearrange("p (c i t) -> p c t i", i=4, t=PACK), src.rearrange("p t (c i) -> p c t i", i=4)
            )

        wa_q = {}
        wc_q = {}
        z_q = {}

        def prepare_wa(g):
            rounded = held("wa_bf%d" % g, [P, PASS * PACK], BF16, "late_bag" if g == 0 else None)
            nc.scalar.copy(
                rounded[:].rearrange("p (t m i) -> p m i t", t=PACK, i=PACK),
                wa_raw[g][:].rearrange("p i (m t) -> p m i t", t=PACK),
            )
            wa_q[g] = quantise("wa%d" % g, rounded[:], PASS)

        def prepare_wc(g):
            rounded = held("wc_bf%d" % g, [P, N * PACK], BF16)
            interleave(rounded[:], wc_raw[g][:])
            wc_q[g] = quantise("wc%d" % g, rounded[:], N)

        units = [(c, g, t0) for c in range(CHUNKS) for g in range(GROUPS) for t0 in range(0, PACK, SLOTS)]

        def adds_on_tensor(n):
            return n >= UNITS_PER_CHUNK and n % 2 == 0

        def turn(n, tiles):
            rank = len([m for m in range(n) if adds_on_tensor(m) == adds_on_tensor(n)])
            return tiles[rank % len(tiles)]

        def airport_of(n):
            c, g, t0 = units[n]
            return airport_sb[c][g][:, t0 : t0 + SLOTS, :].rearrange("p t j -> p (t j)")

        def first_product(n, side, acc):
            c, g, t0 = units[n]
            half, first = divmod(c * CHUNK, HALF)
            for d in range(SLOTS):
                col = (t0 + d) * P
                if side == "bag":
                    weights = wa_q[g][0][:, col : col + P].bitcast(FP8X4)
                    weight_scales = wa_q[g][1][:, col : col + P]
                else:
                    col = g * PASS + col
                    weights = wb_w[:, 2 * col : 2 * (col + P)].bitcast(FP4X4)
                    weight_scales = wb_s[:, col : col + P]
                nc.tensor.matmul_mx(
                    out=acc[:, d * CHUNK : (d + 1) * CHUNK],
                    lhsT=weights,
                    lhsT_scale=weight_scales,
                    rhs=got_words[side, half][:, first : first + CHUNK].bitcast(FP8X4),
                    rhs_scale=got_scales[side, half][:, first : first + CHUNK],
                    start=True,
                    stop=True,
                )

        def scale_and_combine(n, dst, src, other, op):
            c, g, t0 = units[n]
            for d in range(SLOTS):
                cols = slice(d * CHUNK, (d + 1) * CHUNK)
                nc.vector.scalar_tensor_tensor(
                    dst[:, cols], src[:, cols], gain_sb[:, g, t0 + d : t0 + d + 1], other[:, cols], ALU.mult, op
                )

        def stage_reports(n):
            acc = bank_report[n % len(bank_report)]
            first_product(n, "report", acc)
            scale_and_combine(n, ring_reports[n % len(ring_reports)], acc, airport_of(n), ALU.mult)

        def stage_bag_product(n):
            staged = ring_staged[n % len(ring_staged)]
            acc = turn(n, bank_bag_tensor if adds_on_tensor(n) else bank_bag_vector)
            first_product(n, "bag", acc)
            if adds_on_tensor(n):
                nc.scalar.copy(staged[:], acc[:])
            else:
                nc.vector.tensor_tensor(staged[:], acc[:], airport_of(n), ALU.add)

        def stage_tanh(n):
            total = ring_staged[n % len(ring_staged)]
            if adds_on_tensor(n):
                turned = turn(n, bank_turned)
                for first in range(0, BANK, P):
                    cols = slice(first, first + P)
                    for term, opens in ((airport_of(n), True), (total, False)):
                        nc.tensor.matmul(
                            turned[:, cols],
                            lhsT=term[:, cols],
                            rhs=ident[:],
                            start=opens,
                            stop=not opens,
                            is_transpose=True,
                        )
                total = turned
            nc.scalar.activation(ring_bags[n % len(ring_bags)][:], total[:], ACT.Tanh)

        def stage_z(n):
            c, g, t0 = units[n]
            bags = ring_bags[n % len(ring_bags)]
            if adds_on_tensor(n):
                back = turn(n, bank_back)
                for first in range(0, BANK, P):
                    nc.tensor.transpose(back[:, first : first + P], bags[:, first : first + P], ident[:])
                bags = back
            z_unit = ring_z_slots[g][:, t0 : t0 + SLOTS, :].rearrange("p t j -> p (t j)")
            scale_and_combine(n, z_unit, bags, ring_reports[n % len(ring_reports)], ALU.subtract)

        def quantise_z(c, g):
            interleave(ring_z_words[g][:], ring_z_slots[g][:])
            z_q[c, g] = quantise("z%d_%d" % (c, g), ring_z_words[g][:], CHUNK)

        def place(page, chunks, acc, magnitude):
            rows = slice(page * P, (page + 1) * P)
            for d, c in enumerate(chunks):
                for g in range(GROUPS):
                    nc.tensor.matmul_mx(
                        out=acc[:, d * CHUNK : (d + 1) * CHUNK],
                        lhsT=wc_q[g][0][:, rows].bitcast(FP8X4),
                        lhsT_scale=wc_q[g][1][:, rows],
                        rhs=z_q[c, g][0][:].bitcast(FP8X4),
                        rhs_scale=z_q[c, g][1][:],
                        start=(g == 0),
                        stop=(g == GROUPS - 1),
                    )
            start, width = chunks[0] * CHUNK, len(chunks) * CHUNK
            nc.scalar.activation(magnitude, acc[:, 0:width], ACT.Abs)
            window = pages[page][:].indirect(entries(list_out, start, width))
            nc.vector.tensor_tensor(window, magnitude, wgo_sb[:, start : start + width], ALU.mult)

        early = [(page, c) for c in range(CHUNKS // 2) for page in range(PAGES)]

        count = len(units)
        for step in range(count + 2):
            if step < UNITS_PER_CHUNK and units[step][2] == 0:
                prepare_wa(units[step][1])
            if step == 1:
                for side in lists:
                    gather_words(side, 1, shares="late_" + side)
            if 2 <= step < 2 + GROUPS:
                prepare_wc(step - 2)
            if step < count:
                stage_reports(step)
                stage_bag_product(step)
            if 1 <= step <= count:
                stage_tanh(step - 1)
            if step >= 2:
                n = step - 2
                c, g, t0 = units[n]
                stage_z(n)
                if t0 + SLOTS == PACK:
                    quantise_z(c, g)
                    if c > 0:
                        freed = ring_reports[n % len(ring_reports)]
                        spaces = [freed[:, 0:CHUNK]]
                        if n == count - 1:
                            spaces.extend([freed[:, CHUNK:BANK], spare_magnitude[:]])
                        for space in spaces:
                            page, chunk = early[0]
                            early.remove(early[0])
                            place(page, [chunk], bank_y[0], space)

        for page in range(PAGES):
            place(page, range(CHUNKS // 2, CHUNKS), bank_report[page % 2], ring_staged[page % 2][:])
            nc.sync.dma_start(out=out[page * P : (page + 1) * P, :], in_=pages[page][:])
